import numpy as np
CORES = [4,132,260,388,12,140,268,396,20,148,276,404,28,156,284,412]
N = 16
GROUPS = [[0,1,4,5,8,9,12,13],[2,3,6,7,10,11,14,15]]
def setup_inputs(rng):
    return {"x": rng.standard_normal((N, 128, 256), dtype=np.float32)}
def reference(x):
    y = np.empty((N, 128, 32), x.dtype)
    for g in GROUPS:
        s = x[g].sum(axis=0, dtype=np.float64).astype(x[g].dtype)
        n = len(g); b = x.shape[2] // n
        for i, r in enumerate(g):
            y[r] = s[:, i * b:(i + 1) * b]
    return {"y": y}

@@ -1,0 +1,77 @@
+from concourse.bass import DstId, RemoteDMATransfer
+
+SCRATCH = {
+    "xb": ("dram", [8, 128, 32], "float32"),
+    "land": ("dram", [5, 128, 32], "float32"),
+    "res": ("dram", [128, 32], "float32"),
+}
+SEMAPHORES = ["ldc", "lds", "sent", "arr", "res", "stored"]
+
+RANK, FOLD, MATE = 4, 5, 6
+OFF = (0x0003, 0x000C, 0x0030)
+ON = 0xFF00
+N_OFF, N_ON = 2, 8
+
+
+def rank_program(g, core, T, topo):
+    k = core % 8
+    if k not in (RANK, FOLD, MATE):
+        return
+    chip0 = core - k
+    d = (chip0 ^ 8) + RANK if k == MATE else chip0 + RANK
+    r = T.rank_of(d)
+    if r is None:
+        return
+    grp = [m for m in T.tables["GROUPS"] if r in m][0]
+    mem = [T.cores[q] for q in grp]
+    par = topo.chip(core) & 1
+    got = 3 * N_OFF + N_ON
+
+    def fold(srcs, dst_core, dst_ap, sem, mask):
+        rid, pid = topo.addr(dst_core, core)
+        g.remote_dma_fused([RemoteDMATransfer(dst_ids=[DstId(rid=rid, pnc=pid)], dma_engine_mask=mask, remote_sem=sem,
+                                              srcs=srcs, dsts=[dst_ap], alu_op=1)], local_sem=T.sem.sent)
+
+    if k == MATE:
+        g.wait_ge(T.sem.arr, got)
+        fold([T.land[s] for s in range(4)], d - RANK + FOLD, T.land[4], T.sem.arr, 0x00FF)
+        g.wait_ge(T.sem.sent, 8)
+        return
+    if k == FOLD:
+        g.wait_ge(T.sem.arr, got + 8)
+        fold([T.land[s] for s in range(5)], d, T.res[:], T.sem.res, 0xFFFF)
+        g.wait_ge(T.sem.sent, 16)
+        return
+
+    b = T.y.shape[1]
+    same = [j for j, m in enumerate(mem) if (topo.chip(m) & 1) == par]
+    cross = [j for j, m in enumerate(mem) if (topo.chip(m) & 1) != par]
+    slot = same.index(mem.index(core))
+    for blocks, sem in ((cross, T.sem.ldc), (same, T.sem.lds)):
+        for n, j in enumerate(blocks):
+            q = (g.sync, g.scalar)[n % 2]
+            q.dma_start(T.xb[j], T.x[:, j * b:(j + 1) * b]).then_inc(sem, 16)
+
+    def send(blocks, target):
+        trs, off = [], 0
+        for j in blocks:
+            t = target(mem[j])
+            rid, pid = topo.addr(t, core)
+            if t - t % 8 == chip0:
+                mask = ON
+            else:
+                mask = OFF[off]
+                off += 1
+            trs.append(RemoteDMATransfer(dst_ids=[DstId(rid=rid, pnc=pid)], dma_engine_mask=mask, remote_sem=T.sem.arr,
+                                         srcs=[T.xb[j]], dsts=[T.land[slot]], alu_op=0))
+        g.remote_dma_fused(trs, local_sem=T.sem.sent)
+
+    g.wait_ge(T.sem.ldc, 64)
+    send(cross, lambda m: ((m - RANK) ^ 8) + MATE)
+    g.wait_ge(T.sem.lds, 64)
+    send(same, lambda m: m - RANK + FOLD)
+
+    g.sync.wait_ge(T.sem.res, 16)
+    g.sync.dma_start(T.y[:], T.res[:]).then_inc(T.sem.stored, 16)
+    g.wait_ge(T.sem.sent, 2 * got)
+    g.wait_ge(T.sem.stored, 16)

@@ -5,12 +5,28 @@ SCRATCH = {
     "land": ("dram", [5, 128, 32], "float32"),
     "res": ("dram", [128, 32], "float32"),
 }
-SEMAPHORES = ["ldc", "lds", "sent", "arr", "res", "stored"]
+SEMAPHORES = ["ld0", "ld1", "ld2", "sent", "arr", "res", "stored"]
 
 RANK, FOLD, MATE = 4, 5, 6
-OFF = (0x0003, 0x000C, 0x0030)
-ON = 0xFF00
-N_OFF, N_ON = 2, 8
+
+
+def bits(mask):
+    return bin(mask).count("1")
+
+
+def plan(s, mem, topo):
+    par = topo.chip(s) & 1
+    same = [j for j, m in enumerate(mem) if (topo.chip(m) & 1) == par]
+    a = same.index(mem.index(s))
+    chips = [mem[same[(a + n) % 4]] - RANK for n in (1, 2, 3, 0)]
+    blk = {m - RANK: j for j, m in enumerate(mem)}
+    cr = [(blk[c ^ 8], c + MATE) for c in chips]
+    sm = [(blk[c], c + FOLD) for c in chips]
+    return [
+        [cr[0] + (0x000F,), cr[1] + (0x00F0,)],
+        [cr[2] + (0x00FF,), cr[3] + (0xFF00,)],
+        [sm[0] + (0x0003,), sm[1] + (0x000C,), sm[2] + (0x0030,), sm[3] + (0xFF00,)],
+    ]
 
 
 def rank_program(g, core, T, topo):
@@ -25,53 +41,44 @@ def rank_program(g, core, T, topo):
     grp = [m for m in T.tables["GROUPS"] if r in m][0]
     mem = [T.cores[q] for q in grp]
     par = topo.chip(core) & 1
-    got = 3 * N_OFF + N_ON
+    peers = [m for m in mem if (topo.chip(m) & 1) == par]
 
     def fold(srcs, dst_core, dst_ap, sem, mask):
         rid, pid = topo.addr(dst_core, core)
         g.remote_dma_fused([RemoteDMATransfer(dst_ids=[DstId(rid=rid, pnc=pid)], dma_engine_mask=mask, remote_sem=sem,
                                               srcs=srcs, dsts=[dst_ap], alu_op=1)], local_sem=T.sem.sent)
 
-    if k == MATE:
-        g.wait_ge(T.sem.arr, got)
-        fold([T.land[s] for s in range(4)], d - RANK + FOLD, T.land[4], T.sem.arr, 0x00FF)
-        g.wait_ge(T.sem.sent, 8)
-        return
-    if k == FOLD:
-        g.wait_ge(T.sem.arr, got + 8)
-        fold([T.land[s] for s in range(5)], d, T.res[:], T.sem.res, 0xFFFF)
-        g.wait_ge(T.sem.sent, 16)
+    if k != RANK:
+        got = sum(bits(mk) for s in peers for call in plan(s, mem, topo) for (j, t, mk) in call if t == core)
+        if k == MATE:
+            g.wait_ge(T.sem.arr, got)
+            fold([T.land[s] for s in range(4)], d - RANK + FOLD, T.land[4], T.sem.arr, 0x00FF)
+            g.wait_ge(T.sem.sent, 8)
+        else:
+            g.wait_ge(T.sem.arr, got + 8)
+            fold([T.land[s] for s in range(5)], d, T.res[:], T.sem.res, 0xFFFF)
+            g.wait_ge(T.sem.sent, 16)
         return
 
     b = T.y.shape[1]
-    same = [j for j, m in enumerate(mem) if (topo.chip(m) & 1) == par]
-    cross = [j for j, m in enumerate(mem) if (topo.chip(m) & 1) != par]
-    slot = same.index(mem.index(core))
-    for blocks, sem in ((cross, T.sem.ldc), (same, T.sem.lds)):
-        for n, j in enumerate(blocks):
-            q = (g.sync, g.scalar)[n % 2]
-            q.dma_start(T.xb[j], T.x[:, j * b:(j + 1) * b]).then_inc(sem, 16)
-
-    def send(blocks, target):
-        trs, off = [], 0
-        for j in blocks:
-            t = target(mem[j])
+    slot = peers.index(core)
+    calls = plan(core, mem, topo)
+    for n, call in enumerate(calls):
+        for i, (j, t, mk) in enumerate(call):
+            q = (g.sync, g.scalar)[i % 2]
+            q.dma_start(T.xb[j], T.x[:, j * b:(j + 1) * b]).then_inc(T.sem["ld%d" % n], 16)
+    left = 0
+    for n, call in enumerate(calls):
+        trs = []
+        for (j, t, mk) in call:
             rid, pid = topo.addr(t, core)
-            if t - t % 8 == chip0:
-                mask = ON
-            else:
-                mask = OFF[off]
-                off += 1
-            trs.append(RemoteDMATransfer(dst_ids=[DstId(rid=rid, pnc=pid)], dma_engine_mask=mask, remote_sem=T.sem.arr,
+            trs.append(RemoteDMATransfer(dst_ids=[DstId(rid=rid, pnc=pid)], dma_engine_mask=mk, remote_sem=T.sem.arr,
                                          srcs=[T.xb[j]], dsts=[T.land[slot]], alu_op=0))
+            left += bits(mk)
+        g.wait_ge(T.sem["ld%d" % n], 16 * len(call))
         g.remote_dma_fused(trs, local_sem=T.sem.sent)
-
-    g.wait_ge(T.sem.ldc, 64)
-    send(cross, lambda m: ((m - RANK) ^ 8) + MATE)
-    g.wait_ge(T.sem.lds, 64)
-    send(same, lambda m: m - RANK + FOLD)
 
     g.sync.wait_ge(T.sem.res, 16)
     g.sync.dma_start(T.y[:], T.res[:]).then_inc(T.sem.stored, 16)
-    g.wait_ge(T.sem.sent, 2 * got)
+    g.wait_ge(T.sem.sent, left)
     g.wait_ge(T.sem.stored, 16)

from concourse.bass import DstId, RemoteDMATransfer

SCRATCH = {
    "xb": ("dram", [8, 128, 32], "float32"),
    "land": ("dram", [5, 128, 32], "float32"),
    "res": ("dram", [128, 32], "float32"),
}
SEMAPHORES = ["ld0", "ld1", "ld2", "sent", "arr", "res", "stored"]

RANK, FOLD, MATE = 4, 5, 6


def bits(mask):
    return bin(mask).count("1")


def plan(s, mem, topo):
    par = topo.chip(s) & 1
    same = [j for j, m in enumerate(mem) if (topo.chip(m) & 1) == par]
    a = same.index(mem.index(s))
    chips = [mem[same[(a + n) % 4]] - RANK for n in (1, 2, 3, 0)]
    blk = {m - RANK: j for j, m in enumerate(mem)}
    cr = [(blk[c ^ 8], c + MATE) for c in chips]
    sm = [(blk[c], c + FOLD) for c in chips]
    return [
        [cr[0] + (0x000F,), cr[1] + (0x00F0,)],
        [cr[2] + (0x00FF,), cr[3] + (0xFF00,)],
        [sm[0] + (0x0003,), sm[1] + (0x000C,), sm[2] + (0x0030,), sm[3] + (0xFF00,)],
    ]


def rank_program(g, core, T, topo):
    k = core % 8
    if k not in (RANK, FOLD, MATE):
        return
    chip0 = core - k
    d = (chip0 ^ 8) + RANK if k == MATE else chip0 + RANK
    r = T.rank_of(d)
    if r is None:
        return
    grp = [m for m in T.tables["GROUPS"] if r in m][0]
    mem = [T.cores[q] for q in grp]
    par = topo.chip(core) & 1
    peers = [m for m in mem if (topo.chip(m) & 1) == par]

    def fold(srcs, dst_core, dst_ap, sem, mask):
        rid, pid = topo.addr(dst_core, core)
        g.remote_dma_fused([RemoteDMATransfer(dst_ids=[DstId(rid=rid, pnc=pid)], dma_engine_mask=mask, remote_sem=sem,
                                              srcs=srcs, dsts=[dst_ap], alu_op=1)], local_sem=T.sem.sent)

    if k != RANK:
        got = sum(bits(mk) for s in peers for call in plan(s, mem, topo) for (j, t, mk) in call if t == core)
        if k == MATE:
            g.wait_ge(T.sem.arr, got)
            fold([T.land[s] for s in range(4)], d - RANK + FOLD, T.land[4], T.sem.arr, 0x00FF)
            g.wait_ge(T.sem.sent, 8)
        else:
            g.wait_ge(T.sem.arr, got + 8)
            fold([T.land[s] for s in range(5)], d, T.res[:], T.sem.res, 0xFFFF)
            g.wait_ge(T.sem.sent, 16)
        return

    b = T.y.shape[1]
    slot = peers.index(core)
    calls = plan(core, mem, topo)
    for n, call in enumerate(calls):
        for i, (j, t, mk) in enumerate(call):
            q = (g.sync, g.scalar)[i % 2]
            q.dma_start(T.xb[j], T.x[:, j * b:(j + 1) * b]).then_inc(T.sem["ld%d" % n], 16)
    left = 0
    for n, call in enumerate(calls):
        trs = []
        for (j, t, mk) in call:
            rid, pid = topo.addr(t, core)
            trs.append(RemoteDMATransfer(dst_ids=[DstId(rid=rid, pnc=pid)], dma_engine_mask=mk, remote_sem=T.sem.arr,
                                         srcs=[T.xb[j]], dsts=[T.land[slot]], alu_op=0))
            left += bits(mk)
        g.wait_ge(T.sem["ld%d" % n], 16 * len(call))
        g.remote_dma_fused(trs, local_sem=T.sem.sent)

    g.sync.wait_ge(T.sem.res, 16)
    g.sync.dma_start(T.y[:], T.res[:]).then_inc(T.sem.stored, 16)
    g.wait_ge(T.sem.sent, left)
    g.wait_ge(T.sem.stored, 16)
